import numpy as np
import ml_dtypes

BF16 = ml_dtypes.bfloat16


def bf(x):
    return np.asarray(x, np.float32).astype(BF16)


def f32(x):
    return np.asarray(x, np.float32)


def f64(x):
    return np.asarray(x).astype(np.float64)


def striped(idx):
    return np.tile(idx.reshape(-1, 16).T, (8, 1))


S, K, M, N, B, Q = 512, 512, 128, 512, 4, 128


def setup_inputs():
    return {"base": bf(np.random.standard_normal((B, M, S))), "x": bf(np.random.standard_normal((K, N))), "w": bf(np.random.standard_normal((K, M)) / np.sqrt(K)), "offs": striped(np.random.permutation(S))}


def reference(base, x, w, offs):
    idx = offs[:16].T.reshape(-1)
    z = f64(base).copy()
    for i in range(B):
        z[i][:, idx[i * Q : (i + 1) * Q]] += f64(w).T @ f64(x)[:, i * Q : (i + 1) * Q]
    return z

@@ -1,0 +1,55 @@
+import concourse.mybir as mybir
+from concourse.masks import make_identity
+
+BF16, F32, U16 = mybir.dt.bfloat16, mybir.dt.float32, mybir.dt.uint16
+
+P = 128
+B, S = 4, 512
+K, N = 512, 512
+Q = N // B
+KB = K // P
+OC = Q // 16
+
+FLOPS = 2 * K * P * N
+
+
+def tile_scatter_matmul_kernel(tc, base, x, w, offs, out):
+    nc = tc.nc
+    with (
+        tc.tile_pool(name="held", bufs=1) as held,
+        tc.psum_pool(name="windows", bufs=1) as windows,
+    ):
+        base_sb = held.tile([P, B, S], BF16, name="base_sb")
+        offs_sb = held.tile([P, N // 16], U16, name="offs_sb")
+        w_sb = held.tile([P, KB, P], BF16, name="w_sb")
+        x_sb = held.tile([P, KB, N], BF16, name="x_sb")
+        ident = held.tile([P, P], BF16, name="ident")
+
+        nc.sync.dma_start(base_sb[:], base.rearrange("i m s -> m i s"))
+        nc.sync.dma_start(offs_sb[:], offs)
+        nc.sync.dma_start(w_sb[:], w.rearrange("(p b) m -> p b m", b=KB))
+        nc.sync.dma_start(x_sb[:], x.rearrange("(p b) n -> p b n", b=KB))
+        make_identity(nc, ident[:])
+
+        window = [windows.tile([P, S], F32, name=f"window{i}") for i in range(B)]
+        for i in range(B):
+            nc.tensor.matmul(window[i][:], ident[:], base_sb[:, i, :], start=True, stop=False)
+
+        for i in range(B):
+            places = offs_sb[:, i * OC : (i + 1) * OC]
+            for b in range(KB):
+                nc.tensor.matmul(
+                    window[i][:].indirect(places),
+                    w_sb[:, b, :],
+                    x_sb[:, b, i * Q : (i + 1) * Q],
+                    start=False,
+                    stop=b == KB - 1,
+                )
+
+        for i in range(B):
+            z = held.tile([P, S], F32, name=f"z{i}")
+            if i % 2 == 0:
+                nc.vector.tensor_copy(z[:], window[i][:])
+            else:
+                nc.scalar.copy(z[:], window[i][:])
+            nc.sync.dma_start(out[i], z[:])

@@ -10,6 +10,8 @@ Q = N // B
 KB = K // P
 OC = Q // 16
 
+WARM_UP = 4
+
 FLOPS = 2 * K * P * N
 
 
@@ -19,21 +21,28 @@ def tile_scatter_matmul_kernel(tc, base, x, w, offs, out):
         tc.tile_pool(name="held", bufs=1) as held,
         tc.psum_pool(name="windows", bufs=1) as windows,
     ):
-        base_sb = held.tile([P, B, S], BF16, name="base_sb")
+        base_sb = [held.tile([P, S], BF16, name=f"base_sb{i}") for i in range(B)]
         offs_sb = held.tile([P, N // 16], U16, name="offs_sb")
         w_sb = held.tile([P, KB, P], BF16, name="w_sb")
         x_sb = held.tile([P, KB, N], BF16, name="x_sb")
         ident = held.tile([P, P], BF16, name="ident")
 
-        nc.sync.dma_start(base_sb[:], base.rearrange("i m s -> m i s"))
+        for i in range(B):
+            nc.sync.dma_start(base_sb[i][:], base[i])
         nc.sync.dma_start(offs_sb[:], offs)
         nc.sync.dma_start(w_sb[:], w.rearrange("(p b) m -> p b m", b=KB))
         nc.sync.dma_start(x_sb[:], x.rearrange("(p b) n -> p b n", b=KB))
         make_identity(nc, ident[:])
 
+        zeros = held.tile([P, S], BF16, name="zeros")
+        nc.vector.memset(zeros[:], 0.0)
+        spare = windows.tile([P, S], F32, name="spare")
+        for u in range(WARM_UP):
+            nc.tensor.matmul(spare[:], zeros[:, 0:P], zeros[:], start=True, stop=True)
+
         window = [windows.tile([P, S], F32, name=f"window{i}") for i in range(B)]
         for i in range(B):
-            nc.tensor.matmul(window[i][:], ident[:], base_sb[:, i, :], start=True, stop=False)
+            nc.tensor.matmul(window[i][:], ident[:], base_sb[i][:], start=True, stop=False)
 
         for i in range(B):
             places = offs_sb[:, i * OC : (i + 1) * OC]

@@ -8,6 +8,7 @@ B, S = 4, 512
 K, N = 512, 512
 Q = N // B
 KB = K // P
+HB = KB // 2
 OC = Q // 16
 
 WARM_UP = 4
@@ -24,14 +25,16 @@ def tile_scatter_matmul_kernel(tc, base, x, w, offs, out):
         base_sb = [held.tile([P, S], BF16, name=f"base_sb{i}") for i in range(B)]
         offs_sb = held.tile([P, N // 16], U16, name="offs_sb")
         w_sb = held.tile([P, KB, P], BF16, name="w_sb")
-        x_sb = held.tile([P, KB, N], BF16, name="x_sb")
+        x_sb = [held.tile([P, HB, N], BF16, name=f"x_sb{h}") for h in range(2)]
         ident = held.tile([P, P], BF16, name="ident")
 
         for i in range(B):
             nc.sync.dma_start(base_sb[i][:], base[i])
         nc.sync.dma_start(offs_sb[:], offs)
         nc.sync.dma_start(w_sb[:], w.rearrange("(p b) m -> p b m", b=KB))
-        nc.sync.dma_start(x_sb[:], x.rearrange("(p b) n -> p b n", b=KB))
+        x_blocks = x.rearrange("(p b) n -> p b n", b=KB)
+        for h in range(2):
+            nc.sync.dma_start(x_sb[h][:], x_blocks[:, h * HB : (h + 1) * HB, :])
         make_identity(nc, ident[:])
 
         zeros = held.tile([P, S], BF16, name="zeros")
@@ -50,7 +53,7 @@ def tile_scatter_matmul_kernel(tc, base, x, w, offs, out):
                 nc.tensor.matmul(
                     window[i][:].indirect(places),
                     w_sb[:, b, :],
-                    x_sb[:, b, i * Q : (i + 1) * Q],
+                    x_sb[b // HB][:, b % HB, i * Q : (i + 1) * Q],
                     start=False,
                     stop=b == KB - 1,
                 )

@@ -9,6 +9,7 @@ K, N = 512, 512
 Q = N // B
 KB = K // P
 HB = KB // 2
+SH = S // 2
 OC = Q // 16
 
 WARM_UP = 4
@@ -59,9 +60,12 @@ def tile_scatter_matmul_kernel(tc, base, x, w, offs, out):
                 )
 
         for i in range(B):
-            z = held.tile([P, S], F32, name=f"z{i}")
-            if i % 2 == 0:
-                nc.vector.tensor_copy(z[:], window[i][:])
-            else:
-                nc.scalar.copy(z[:], window[i][:])
-            nc.sync.dma_start(out[i], z[:])
+            for c in range(2):
+                z = held.tile([P, SH], F32, name=f"z{i}_{c}")
+                half = window[i][:, c * SH : (c + 1) * SH]
+                if i % 2 == 0:
+                    nc.vector.tensor_copy(z[:], half)
+                    nc.sync.dma_start(out[i, :, c * SH : (c + 1) * SH], z[:])
+                else:
+                    nc.scalar.copy(z[:], half)
+                    nc.scalar.dma_start(out[i, :, c * SH : (c + 1) * SH], z[:])

import concourse.mybir as mybir
from concourse.masks import make_identity

BF16, F32, U16 = mybir.dt.bfloat16, mybir.dt.float32, mybir.dt.uint16

P = 128
B, S = 4, 512
K, N = 512, 512
Q = N // B
KB = K // P
HB = KB // 2
SH = S // 2
OC = Q // 16

WARM_UP = 4

FLOPS = 2 * K * P * N


def tile_scatter_matmul_kernel(tc, base, x, w, offs, out):
    nc = tc.nc
    with (
        tc.tile_pool(name="held", bufs=1) as held,
        tc.psum_pool(name="windows", bufs=1) as windows,
    ):
        base_sb = [held.tile([P, S], BF16, name=f"base_sb{i}") for i in range(B)]
        offs_sb = held.tile([P, N // 16], U16, name="offs_sb")
        w_sb = held.tile([P, KB, P], BF16, name="w_sb")
        x_sb = [held.tile([P, HB, N], BF16, name=f"x_sb{h}") for h in range(2)]
        ident = held.tile([P, P], BF16, name="ident")

        for i in range(B):
            nc.sync.dma_start(base_sb[i][:], base[i])
        nc.sync.dma_start(offs_sb[:], offs)
        nc.sync.dma_start(w_sb[:], w.rearrange("(p b) m -> p b m", b=KB))
        x_blocks = x.rearrange("(p b) n -> p b n", b=KB)
        for h in range(2):
            nc.sync.dma_start(x_sb[h][:], x_blocks[:, h * HB : (h + 1) * HB, :])
        make_identity(nc, ident[:])

        zeros = held.tile([P, S], BF16, name="zeros")
        nc.vector.memset(zeros[:], 0.0)
        spare = windows.tile([P, S], F32, name="spare")
        for u in range(WARM_UP):
            nc.tensor.matmul(spare[:], zeros[:, 0:P], zeros[:], start=True, stop=True)

        window = [windows.tile([P, S], F32, name=f"window{i}") for i in range(B)]
        for i in range(B):
            nc.tensor.matmul(window[i][:], ident[:], base_sb[i][:], start=True, stop=False)

        for i in range(B):
            places = offs_sb[:, i * OC : (i + 1) * OC]
            for b in range(KB):
                nc.tensor.matmul(
                    window[i][:].indirect(places),
                    w_sb[:, b, :],
                    x_sb[b // HB][:, b % HB, i * Q : (i + 1) * Q],
                    start=False,
                    stop=b == KB - 1,
                )

        for i in range(B):
            for c in range(2):
                z = held.tile([P, SH], F32, name=f"z{i}_{c}")
                half = window[i][:, c * SH : (c + 1) * SH]
                if i % 2 == 0:
                    nc.vector.tensor_copy(z[:], half)
                    nc.sync.dma_start(out[i, :, c * SH : (c + 1) * SH], z[:])
                else:
                    nc.scalar.copy(z[:], half)
                    nc.scalar.dma_start(out[i, :, c * SH : (c + 1) * SH], z[:])
